import numpy as np
import ml_dtypes


def mxq(x, axis, fmt="e4m3"):
    dtype, down = {"e4m3": (ml_dtypes.float8_e4m3fn, 7), "e5m2": (ml_dtypes.float8_e5m2, 14)}[fmt]
    v = np.moveaxis(np.asarray(x, np.float32).astype(ml_dtypes.bfloat16).astype(np.float64), axis, -1)
    blocks = v.reshape(v.shape[:-1] + (-1, 32))
    amax = np.abs(blocks).max(-1, keepdims=True)
    byte = np.maximum(np.where(amax > 0, np.frexp(amax)[1] - 1 + 127, 0) - down, 1)
    scale = np.exp2(byte - 127.0)
    codes = (blocks / scale).astype(np.float32).astype(dtype).astype(np.float64)
    return np.moveaxis((codes * scale).reshape(v.shape), -1, axis)


WIDE = False


def mx_kscale(k):
    if not WIDE:
        return np.ones(k)
    levels = np.array([10, -10, 5, -5, 0])
    if k % 512:
        return np.exp2(np.random.permutation(np.resize(levels, k // 32))).repeat(32)
    a = np.empty((k // 512, 16))
    for p in range(k // 512):
        a[p, :8] = np.random.permutation(np.resize(levels, 8))
        for g in range(8):
            far = levels[np.abs(levels - a[p, g]) >= 10]
            a[p, g + 8] = far[np.random.randint(len(far))]
    return np.exp2(a.ravel()).repeat(32)


def f64(x):
    return np.asarray(x).astype(np.float64)


def striped(idx):
    return np.tile(idx.reshape(-1, 16).T, (8, 1)).astype(np.uint16)


def unstriped(offs):
    return offs[:16].T.reshape(-1).astype(np.int64)


E2M1 = np.array([0.0, 0.5, 1.0, 1.5, 2.0, 3.0, 4.0, 6.0, -0.0, -0.5, -1.0, -1.5, -2.0, -3.0, -4.0, -6.0])


def pack_weight(w, fmt):
    k, n = w.shape
    w = f64(np.asarray(w, np.float32).astype(ml_dtypes.bfloat16)).reshape(k // 32, 32, n)
    amax = np.abs(w).max(1)
    if fmt == "e4m3":
        byte = np.frexp(amax)[1] - 1 + 127 - 7
    else:
        mant, ex = np.frexp(amax / 6.0)
        byte = np.where(mant > 0.5, ex, ex - 1) + 127
    byte = np.clip(np.where(amax > 0, byte, 1), 1, 254)
    scaled = (w * np.exp2(127.0 - byte)[:, None, :]).reshape(k, n).astype(np.float32)
    by_word = np.ascontiguousarray(scaled.reshape(k // 512, 128, 4, n).transpose(0, 1, 3, 2))
    if fmt == "e4m3":
        words = by_word.astype(ml_dtypes.float8_e4m3fn).view(np.uint8)
    else:
        c = by_word.astype(ml_dtypes.float4_e2m1fn).view(np.uint8) & 0xF
        words = (c[..., 0::2] | (c[..., 1::2] << 4)).reshape(k // 512, 128, 2 * n)
    return np.ascontiguousarray(words), np.ascontiguousarray(byte.astype(np.uint8).reshape(k // 512, 16, n))


def unpack_weight(words, scales, fmt):
    g, _, n = scales.shape
    words = np.ascontiguousarray(words).reshape(g, 128, n, -1)
    if fmt == "e4m3":
        vals = words.view(ml_dtypes.float8_e4m3fn).astype(np.float64)
    else:
        nib = np.empty((g, 128, n, 4), np.uint8)
        nib[..., 0::2] = words & 0xF
        nib[..., 1::2] = words >> 4
        vals = E2M1[nib]
    vals = vals * np.repeat(np.exp2(scales.astype(np.float64) - 127.0), 8, axis=1)[..., None]
    return vals.transpose(0, 1, 3, 2).reshape(g * 512, n)


def planes(y):
    n, m = y.shape
    v = y.astype(np.float32).astype(ml_dtypes.bfloat16).astype(np.float64).reshape(n // 32, 32, m)
    top = np.abs(v).max(1)
    byte = np.clip(np.where(top > 0, np.frexp(top)[1] - 1 + 127 - 7, 1), 1, 254)
    codes = (v * np.exp2(127.0 - byte)[:, None, :]).reshape(n, m).astype(np.float32).astype(ml_dtypes.float8_e4m3fn).view(np.uint8)
    words = codes.reshape(n // 512, 128, 4, m).transpose(0, 1, 3, 2)
    return np.ascontiguousarray(words), np.ascontiguousarray(byte.astype(np.uint8).reshape(n // 512, 16, m))


def gelu(v):
    return 0.5 * v * (1.0 + np.tanh(np.sqrt(2.0 / np.pi) * (v + 0.044715 * v**3)))


K, T, E, C, H, N = 512, 768, 12, 128, 512, 512


def by_expert(wq, xq):
    return np.concatenate([wq[e].T @ xq[:, e * C:(e + 1) * C] for e in range(E)], axis=1)


def setup_inputs():
    n = np.random.standard_normal
    s = mx_kscale(K)
    u = mx_kscale(H)
    slot_token = np.concatenate([np.random.permutation(T)[:C] for e in range(E)])
    x = pack_weight(n((K, T)) * s[:, None], "e4m3")
    w = [pack_weight(m, "e2m1") for m in n((E, K, N)) / np.sqrt(K) / s[None, :, None]]
    return {
        "x_words": x[0],
        "x_scales": x[1],
        "w_words": np.stack([m[0] for m in w]),
        "w_scales": np.stack([m[1] for m in w]),
        "wa": (n((E, K, H)) / np.sqrt(K) / s[None, :, None] * u).astype(np.float32),
        "wb": (n((E, H, N)) / np.sqrt(H) / u[None, :, None]).astype(np.float32),
        "offs": striped(slot_token),
    }


def reference(x_words, x_scales, w_words, w_scales, wa, wb, offs):
    w = np.stack([unpack_weight(w_words[e], w_scales[e], "e2m1") for e in range(E)])
    waq = mxq(f64(wa), 1, "e4m3")
    wbq = mxq(f64(wb), 1, "e4m3")
    idx = unstriped(offs)
    xq = unpack_weight(x_words, x_scales, "e4m3")[:, idx]
    h = gelu(by_expert(waq, xq))
    y = by_expert(w, xq) + by_expert(wbq, mxq(h, 0, "e4m3"))
    out = y
    out_0 = out
    return (out_0,) + planes(out_0)

@@ -1,0 +1,297 @@
+from contextlib import ExitStack
+
+import concourse.mybir as mybir
+from concourse.masks import make_identity
+
+K, T, E, C, H, N = 512, 768, 12, 128, 512, 512
+FLOPS = 2 * E * C * (K * H + K * N + H * N)
+
+F32 = mybir.dt.float32
+BF16 = mybir.dt.bfloat16
+I32 = mybir.dt.int32
+U32 = mybir.dt.uint32
+U16 = mybir.dt.uint16
+U8 = mybir.dt.uint8
+FP8X4 = mybir.dt.float8_e4m3fn_x4
+FP4X4 = mybir.dt.float4_e2m1fn_x4
+GELU = mybir.ActivationFunctionType.Gelu_apprx_tanh
+
+P = 128
+PACK = 4
+QUADS = 4
+QUAD = 32
+LIST_COLS = C // 16
+SLOTS = 8
+SLOT_BYTES = PACK * H * 4
+GATHERS = ((0, 4), (4, 8), (8, 9), (9, 10), (10, 11), (11, 12))
+LATE_GATHER_LEAD = 4
+W_LOADS = ((0, 4), (4, 8), (8, 12))
+STORES = ((0, 8), (8, 11), (11, 12))
+PLANE_EXPERTS = 3
+
+
+def span_of(spans, e):
+    return [s for s in spans if s[0] <= e < s[1]][0]
+
+
+def tile_moe_elr_s_gelu_kernel(
+    tc, x_words, x_scales, w_words, w_scales, wa, wb, offs, out_0, out_1, out_2
+):
+    nc = tc.nc
+    with ExitStack() as ctx:
+        keep = ctx.enter_context(tc.tile_pool(name="keep", bufs=1))
+        ring = ctx.enter_context(tc.tile_pool(name="ring", bufs=1))
+        work = ctx.enter_context(tc.tile_pool(name="work", bufs=3))
+        psum_h = ctx.enter_context(tc.psum_pool(name="psum_h", bufs=2))
+        psum_y = ctx.enter_context(tc.psum_pool(name="psum_y", bufs=3))
+
+        offsets = keep.tile([P, E * LIST_COLS], U16, name="offsets")
+        tok_words = keep.tile([P, T], U32, name="tok_words", align_bytes=64)
+        tok_scales = keep.tile([P, T], U8, name="tok_scales", align_bytes=64)
+        w_planes = keep.tile([P, E, N], U8, name="w_planes", align_bytes=64)
+        ident = keep.tile([P, P], F32, name="ident")
+        y_planes = keep.tile([P, PLANE_EXPERTS * C], U8, name="y_planes", align_bytes=64)
+
+        nc.gpsimd.memset(tok_scales[:].bitcast(I32), 0)
+        nc.vector.memset(w_planes[:].bitcast(I32), 0)
+        make_identity(nc, ident[:])
+
+        wa_raw, wb_raw, w_codes = {}, {}, {}
+
+        def in_slot(side, e, shape, dtype, name, at):
+            slot = 2 * (e % SLOTS) + side
+            return ring.tile(
+                shape, dtype, name="%s_%d" % (name, slot), align_bytes=64, offset=slot * SLOT_BYTES + at
+            )
+
+        def load_wa(e):
+            wa_raw[e] = in_slot(0, e, [P, PACK, H], F32, "wa_raw", 0)
+            nc.sync.dma_start(out=wa_raw[e][:], in_=wa[e].rearrange("(p j) i -> p j i", j=PACK))
+
+        def load_wb(e):
+            wb_raw[e] = in_slot(1, e, [P, PACK, N], F32, "wb_raw", 0)
+            nc.sync.dma_start(out=wb_raw[e][:], in_=wb[e].rearrange("(p j) n -> p j n", j=PACK))
+
+        def load_w(span):
+            first, last = span
+            w_codes[span] = keep.tile([P, last - first, 2 * N], U8, name="w_codes_%d" % first, align_bytes=64)
+            nc.sync.dma_start(
+                out=w_codes[span][:].bitcast(I32),
+                in_=w_words[first:last, 0].rearrange("e p b -> p e b").bitcast(I32),
+            )
+
+        def load_expert(e):
+            load_wb(e)
+            load_wa(e)
+            if span_of(W_LOADS, e)[0] == e:
+                load_w(span_of(W_LOADS, e))
+
+        nc.sync.dma_start(offsets[:], offs)
+        nc.sync.dma_start(
+            out=tok_words[:].bitcast(I32), in_=x_words[0].rearrange("p t d -> p (t d)").bitcast(I32)
+        )
+        for q in range(QUADS):
+            nc.scalar.dma_start(
+                out=tok_scales[QUAD * q : QUAD * q + 4, :].bitcast(I32),
+                in_=x_scales[0, 4 * q : 4 * q + 4, :].bitcast(I32),
+            )
+        load_expert(0)
+        for q in range(QUADS):
+            nc.sync.dma_start(
+                out=w_planes[QUAD * q : QUAD * q + 4].bitcast(I32),
+                in_=w_scales[:, 0, 4 * q : 4 * q + 4, :].rearrange("e r n -> r e n").bitcast(I32),
+            )
+        for e in range(1, SLOTS):
+            load_expert(e)
+
+        slot_words, slot_scales = {}, {}
+
+        def gather(span):
+            first, last = span
+            width = (last - first) * C
+            picks = offsets[:, first * LIST_COLS : last * LIST_COLS]
+            if first < SLOTS:
+                slot_words[span] = keep.tile([P, width], U32, name="slot_words_%d" % first, align_bytes=64)
+                slot_scales[span] = keep.tile([P, width], U8, name="slot_scales_%d" % first, align_bytes=64)
+            else:
+                slot_words[span] = in_slot(0, first - LATE_GATHER_LEAD, [P, width], U32, "slot_words", 5120)
+                slot_scales[span] = in_slot(0, first - LATE_GATHER_LEAD, [P, width], U8, "slot_scales", 5632)
+            nc.vector.tensor_copy(slot_words[span][:], tok_words[:].indirect(picks))
+            nc.vector.tensor_copy(slot_scales[span][:], tok_scales[:].indirect(picks))
+
+        def slots_of(e):
+            span = span_of(GATHERS, e)
+            cols = slice((e - span[0]) * C, (e - span[0] + 1) * C)
+            return slot_words[span][:, cols].bitcast(FP8X4), slot_scales[span][:, cols]
+
+        wa_bf, wb_bf, h_bf, y_bf = {}, {}, {}, {}
+        wa_q, wb_q, h_q = {}, {}, {}
+        pre, y_rows, y_cols = {}, {}, {}
+        y_f32, y_codes = {}, {}
+
+        def quantize(values, codes, scales):
+            nc.vector.quantize_mx(out=codes[:].bitcast(FP8X4), scales=scales[:], in_=values[:])
+            return codes, scales
+
+        def cast_wa(e):
+            wa_bf[e] = work.tile([P, PACK * H], BF16, name="wa_bf", align_bytes=64)
+            nc.vector.tensor_copy(
+                out=wa_bf[e][:].rearrange("p (t m j) -> p m j t", t=PACK, j=PACK),
+                in_=wa_raw[e][:].rearrange("p j (m t) -> p m j t", t=PACK),
+            )
+
+        def cast_wb(e):
+            wb_bf[e] = work.tile([P, PACK * N], BF16, name="wb_bf", align_bytes=64)
+            nc.scalar.copy(
+                out=wb_bf[e][:].rearrange("p (c i j) -> p c j i", i=4, j=PACK),
+                in_=wb_raw[e][:].rearrange("p j (c i) -> p c j i", i=4),
+            )
+
+        def quantize_wa(e):
+            codes = work.tile([P, H], U32, name="wa_codes", align_bytes=64)
+            scales = work.tile([P, H], U8, name="wa_scales", align_bytes=64)
+            wa_q[e] = quantize(wa_bf[e], codes, scales)
+
+        def quantize_wb(e):
+            codes = in_slot(0, e, [P, N], U32, "wb_codes", 0)
+            scales = in_slot(0, e, [P, N], U8, "wb_scales", 2048)
+            wb_q[e] = quantize(wb_bf[e], codes, scales)
+
+        def quantize_h(e):
+            codes = in_slot(0, e + 1, [P, C], U32, "h_codes", 2560)
+            scales = in_slot(0, e + 1, [P, C], U8, "h_scales", 3072)
+            h_q[e] = quantize(h_bf[e], codes, scales)
+
+        def first_product(e):
+            x_codes, x_plane = slots_of(e)
+            codes, scales = wa_q[e]
+            pre[e] = psum_h.tile([P, PACK, C], F32, name="pre")
+            for t in range(PACK):
+                cols = slice(t * P, (t + 1) * P)
+                nc.tensor.matmul_mx(
+                    out=pre[e][:, t, :],
+                    lhsT=codes[:, cols].bitcast(FP8X4),
+                    lhsT_scale=scales[:, cols],
+                    rhs=x_codes,
+                    rhs_scale=x_plane,
+                    start=True,
+                    stop=True,
+                )
+
+        def gelu(e):
+            h_bf[e] = in_slot(1, e + 1, [P, C * PACK], BF16, "h_bf", 0)
+            nc.scalar.activation(
+                out=h_bf[e][:].rearrange("p (u t) -> p u t", t=PACK),
+                in_=pre[e][:].rearrange("p t u -> p u t"),
+                func=GELU,
+            )
+
+        def second_product(e):
+            x_codes, x_plane = slots_of(e)
+            w_span = span_of(W_LOADS, e)
+            y_rows[e] = psum_y.tile([C, N], F32, name="y_rows")
+            nc.tensor.matmul_mx(
+                out=y_rows[e][:],
+                lhsT=x_codes,
+                lhsT_scale=x_plane,
+                rhs=w_codes[w_span][:, e - w_span[0], :].bitcast(FP4X4),
+                rhs_scale=w_planes[:, e, :],
+                start=True,
+                stop=False,
+            )
+            nc.tensor.matmul_mx(
+                out=y_rows[e][:],
+                lhsT=h_q[e][0][:].bitcast(FP8X4),
+                lhsT_scale=h_q[e][1][:],
+                rhs=wb_q[e][0][:].bitcast(FP8X4),
+                rhs_scale=wb_q[e][1][:],
+                start=False,
+                stop=True,
+            )
+
+        def turn(e):
+            y_dealt = in_slot(1, e + 2, [C, PACK, P], F32, "y_dealt", 1024)
+            nc.scalar.copy(out=y_dealt[:], in_=y_rows[e][:].rearrange("u (m t) -> u t m", t=PACK))
+            y_cols[e] = psum_y.tile([P, PACK, C], F32, name="y_cols")
+            for t in range(PACK):
+                nc.tensor.transpose(y_cols[e][:, t, :], y_dealt[:, t, :], ident[:])
+
+        def store_cols(e):
+            span = span_of(STORES, e)
+            return span, slice((e - span[0]) * C, (e - span[0] + 1) * C)
+
+        def empty(e):
+            span, cols = store_cols(e)
+            first, last = span
+            if e == first:
+                width = (last - first) * C
+                y_f32[span] = keep.tile([P, PACK, width], F32, name="y_f32_%d" % first)
+                y_codes[span] = keep.tile([P, width], U32, name="y_codes_%d" % first, align_bytes=64)
+            nc.scalar.copy(out=y_f32[span][:, :, cols], in_=y_cols[e][:])
+            if e == last - 1:
+                nc.sync.dma_start(
+                    out=out_0.rearrange("(p t) j -> p t j", t=PACK)[:, :, first * C : last * C],
+                    in_=y_f32[span][:],
+                )
+
+        def cast_y(e):
+            span, cols = store_cols(e)
+            y_bf[e] = in_slot(0, e + 2, [P, C * PACK], BF16, "y_bf", 4096)
+            nc.vector.tensor_copy(
+                out=y_bf[e][:].rearrange("p (c i t) -> p c t i", i=4, t=PACK),
+                in_=y_f32[span][:, :, cols].rearrange("p t (c i) -> p c t i", i=4),
+            )
+
+        def quantize_y(e):
+            span, cols = store_cols(e)
+            first, last = span
+            a, b = divmod(e, PLANE_EXPERTS)
+            nc.vector.quantize_mx(
+                out=y_codes[span][:, cols].bitcast(FP8X4),
+                scales=y_planes[4 * a : P, b * C : (b + 1) * C],
+                in_=y_bf[e][:],
+            )
+            if e == last - 1:
+                nc.sync.dma_start(
+                    out=out_1[0].rearrange("p j d -> p (j d)").bitcast(I32)[:, first * C : last * C],
+                    in_=y_codes[span][:].bitcast(I32),
+                )
+
+        def late_gather(e):
+            if e >= SLOTS:
+                gather(span_of(GATHERS, e))
+
+        for span in GATHERS:
+            if span[0] < SLOTS:
+                gather(span)
+        cast_wb(0)
+
+        stages = (
+            (cast_wa, 0),
+            (quantize_wb, 0),
+            (quantize_h, 1),
+            (second_product, 1),
+            (cast_y, 2),
+            (quantize_wa, 0),
+            (first_product, 0),
+            (quantize_y, 2),
+            (late_gather, -LATE_GATHER_LEAD),
+            (cast_wb, -1),
+            (turn, 1),
+            (gelu, 0),
+            (empty, 1),
+        )
+        for step in range(E + 2):
+            for stage, lag in stages:
+                if 0 <= step - lag < E and not (stage is cast_wb and step - lag == 0):
+                    stage(step - lag)
+            if 1 <= step and step - 1 + SLOTS < E:
+                load_expert(step - 1 + SLOTS)
+
+        for q in range(QUADS):
+            nc.sync.dma_start(
+                out=out_2[0, 4 * q : 4 * q + 4, :]
+                .rearrange("r (a w) -> a r w", a=E // PLANE_EXPERTS)
+                .bitcast(I32),
+                in_=y_planes[QUAD * q : QUAD * q + 16, :].bitcast(I32),
+            )

@@ -22,11 +22,13 @@ QUADS = 4
 QUAD = 32
 LIST_COLS = C // 16
 SLOTS = 8
-SLOT_BYTES = PACK * H * 4
+AT_H_BF, AT_Y_DEALT, AT_Y_BF, AT_WB_SCALES, AT_WORDS, AT_SCALES, AT_WB_BF = 0, 1024, 3072, 4096, 4608, 5120, 5248
+SLOT_BYTES = AT_WB_BF + PACK * N * 2
 GATHERS = ((0, 4), (4, 8), (8, 9), (9, 10), (10, 11), (11, 12))
 LATE_GATHER_LEAD = 4
+LAST_CUT = 44
 W_LOADS = ((0, 4), (4, 8), (8, 12))
-STORES = ((0, 8), (8, 11), (11, 12))
+STORES = ((0, 8), (8, 10), (10, 12))
 PLANE_EXPERTS = 3
 
 
@@ -41,6 +43,7 @@ def tile_moe_elr_s_gelu_kernel(
     with ExitStack() as ctx:
         keep = ctx.enter_context(tc.tile_pool(name="keep", bufs=1))
         ring = ctx.enter_context(tc.tile_pool(name="ring", bufs=1))
+        wb_pool = ctx.enter_context(tc.tile_pool(name="wb_pool", bufs=SLOTS))
         work = ctx.enter_context(tc.tile_pool(name="work", bufs=3))
         psum_h = ctx.enter_context(tc.psum_pool(name="psum_h", bufs=2))
         psum_y = ctx.enter_context(tc.psum_pool(name="psum_y", bufs=3))
@@ -58,18 +61,18 @@ def tile_moe_elr_s_gelu_kernel(
 
         wa_raw, wb_raw, w_codes = {}, {}, {}
 
-        def in_slot(side, e, shape, dtype, name, at):
-            slot = 2 * (e % SLOTS) + side
+        def in_slot(e, shape, dtype, name, at):
+            slot = e % SLOTS
             return ring.tile(
                 shape, dtype, name="%s_%d" % (name, slot), align_bytes=64, offset=slot * SLOT_BYTES + at
             )
 
         def load_wa(e):
-            wa_raw[e] = in_slot(0, e, [P, PACK, H], F32, "wa_raw", 0)
+            wa_raw[e] = in_slot(e, [P, PACK, H], F32, "wa_raw", 0)
             nc.sync.dma_start(out=wa_raw[e][:], in_=wa[e].rearrange("(p j) i -> p j i", j=PACK))
 
         def load_wb(e):
-            wb_raw[e] = in_slot(1, e, [P, PACK, N], F32, "wb_raw", 0)
+            wb_raw[e] = wb_pool.tile([P, PACK, N], F32, name="wb_raw")
             nc.sync.dma_start(out=wb_raw[e][:], in_=wb[e].rearrange("(p j) n -> p j n", j=PACK))
 
         def load_w(span):
@@ -81,8 +84,12 @@ def tile_moe_elr_s_gelu_kernel(
             )
 
         def load_expert(e):
-            load_wb(e)
-            load_wa(e)
+            if e < E - 1:
+                load_wb(e)
+                load_wa(e)
+            else:
+                load_wa(e)
+                load_wb(e)
             if span_of(W_LOADS, e)[0] == e:
                 load_w(span_of(W_LOADS, e))
 
@@ -114,8 +121,8 @@ def tile_moe_elr_s_gelu_kernel(
                 slot_words[span] = keep.tile([P, width], U32, name="slot_words_%d" % first, align_bytes=64)
                 slot_scales[span] = keep.tile([P, width], U8, name="slot_scales_%d" % first, align_bytes=64)
             else:
-                slot_words[span] = in_slot(0, first - LATE_GATHER_LEAD, [P, width], U32, "slot_words", 5120)
-                slot_scales[span] = in_slot(0, first - LATE_GATHER_LEAD, [P, width], U8, "slot_scales", 5632)
+                slot_words[span] = in_slot(first - LATE_GATHER_LEAD, [P, width], U32, "slot_words", AT_WORDS)
+                slot_scales[span] = in_slot(first - LATE_GATHER_LEAD, [P, width], U8, "slot_scales", AT_SCALES)
             nc.vector.tensor_copy(slot_words[span][:], tok_words[:].indirect(picks))
             nc.vector.tensor_copy(slot_scales[span][:], tok_scales[:].indirect(picks))
 
@@ -136,16 +143,19 @@ def tile_moe_elr_s_gelu_kernel(
         def cast_wa(e):
             wa_bf[e] = work.tile([P, PACK * H], BF16, name="wa_bf", align_bytes=64)
             nc.vector.tensor_copy(
-                out=wa_bf[e][:].rearrange("p (t m j) -> p m j t", t=PACK, j=PACK),
-                in_=wa_raw[e][:].rearrange("p j (m t) -> p m j t", t=PACK),
+                out=wa_bf[e][:].rearrange("p (t m j) -> p m t j", t=PACK, j=PACK),
+                in_=wa_raw[e][:].rearrange("p j (m t) -> p m t j", t=PACK),
             )
 
         def cast_wb(e):
-            wb_bf[e] = work.tile([P, PACK * N], BF16, name="wb_bf", align_bytes=64)
-            nc.scalar.copy(
-                out=wb_bf[e][:].rearrange("p (c i j) -> p c j i", i=4, j=PACK),
-                in_=wb_raw[e][:].rearrange("p j (c i) -> p c j i", i=4),
-            )
+            wb_bf[e] = in_slot(e, [P, PACK * N], BF16, "wb_bf", AT_WB_BF)
+            grouped = wb_bf[e][:].rearrange("p (c i j) -> p c j i", i=4, j=PACK)
+            rows = wb_raw[e][:].rearrange("p j (c i) -> p c j i", i=4)
+            if e < E - 1:
+                nc.scalar.copy(out=grouped, in_=rows)
+            else:
+                nc.scalar.copy(out=grouped[:, :LAST_CUT], in_=rows[:, :LAST_CUT])
+                nc.vector.tensor_copy(out=grouped[:, LAST_CUT:], in_=rows[:, LAST_CUT:])
 
         def quantize_wa(e):
             codes = work.tile([P, H], U32, name="wa_codes", align_bytes=64)
@@ -153,13 +163,13 @@ def tile_moe_elr_s_gelu_kernel(
             wa_q[e] = quantize(wa_bf[e], codes, scales)
 
         def quantize_wb(e):
-            codes = in_slot(0, e, [P, N], U32, "wb_codes", 0)
-            scales = in_slot(0, e, [P, N], U8, "wb_scales", 2048)
+            codes = work.tile([P, N], U32, name="wb_codes", align_bytes=64)
+            scales = in_slot(e + 1, [P, N], U8, "wb_scales", AT_WB_SCALES)
             wb_q[e] = quantize(wb_bf[e], codes, scales)
 
         def quantize_h(e):
-            codes = in_slot(0, e + 1, [P, C], U32, "h_codes", 2560)
-            scales = in_slot(0, e + 1, [P, C], U8, "h_scales", 3072)
+            codes = work.tile([P, C], U32, name="h_codes", align_bytes=64)
+            scales = work.tile([P, C], U8, name="h_scales", align_bytes=64)
             h_q[e] = quantize(h_bf[e], codes, scales)
 
         def first_product(e):
@@ -179,7 +189,7 @@ def tile_moe_elr_s_gelu_kernel(
                 )
 
         def gelu(e):
-            h_bf[e] = in_slot(1, e + 1, [P, C * PACK], BF16, "h_bf", 0)
+            h_bf[e] = in_slot(e + 1, [P, C * PACK], BF16, "h_bf", AT_H_BF)
             nc.scalar.activation(
                 out=h_bf[e][:].rearrange("p (u t) -> p u t", t=PACK),
                 in_=pre[e][:].rearrange("p t u -> p u t"),
@@ -210,7 +220,7 @@ def tile_moe_elr_s_gelu_kernel(
             )
 
         def turn(e):
-            y_dealt = in_slot(1, e + 2, [C, PACK, P], F32, "y_dealt", 1024)
+            y_dealt = in_slot(e + 2, [C, PACK, P], F32, "y_dealt", AT_Y_DEALT)
             nc.scalar.copy(out=y_dealt[:], in_=y_rows[e][:].rearrange("u (m t) -> u t m", t=PACK))
             y_cols[e] = psum_y.tile([P, PACK, C], F32, name="y_cols")
             for t in range(PACK):
@@ -236,7 +246,7 @@ def tile_moe_elr_s_gelu_kernel(
 
         def cast_y(e):
             span, cols = store_cols(e)
-            y_bf[e] = in_slot(0, e + 2, [P, C * PACK], BF16, "y_bf", 4096)
+            y_bf[e] = in_slot(e + 3, [P, C * PACK], BF16, "y_bf", AT_Y_BF)
             nc.vector.tensor_copy(
                 out=y_bf[e][:].rearrange("p (c i t) -> p c t i", i=4, t=PACK),
                 in_=y_f32[span][:, :, cols].rearrange("p t (c i) -> p c t i", i=4),
@@ -264,26 +274,25 @@ def tile_moe_elr_s_gelu_kernel(
         for span in GATHERS:
             if span[0] < SLOTS:
                 gather(span)
-        cast_wb(0)
 
         stages = (
             (cast_wa, 0),
-            (quantize_wb, 0),
+            (gelu, 1),
+            (turn, 2),
+            (cast_wb, 0),
+            (empty, 2),
+            (quantize_wb, 1),
+            (cast_y, 3),
             (quantize_h, 1),
             (second_product, 1),
-            (cast_y, 2),
             (quantize_wa, 0),
             (first_product, 0),
-            (quantize_y, 2),
+            (quantize_y, 3),
             (late_gather, -LATE_GATHER_LEAD),
-            (cast_wb, -1),
-            (turn, 1),
-            (gelu, 0),
-            (empty, 1),
         )
-        for step in range(E + 2):
+        for step in range(E + 3):
             for stage, lag in stages:
-                if 0 <= step - lag < E and not (stage is cast_wb and step - lag == 0):
+                if 0 <= step - lag < E:
                     stage(step - lag)
             if 1 <= step and step - 1 + SLOTS < E:
                 load_expert(step - 1 + SLOTS)

@@ -26,8 +26,9 @@ AT_H_BF, AT_Y_DEALT, AT_Y_BF, AT_WB_SCALES, AT_WORDS, AT_SCALES, AT_WB_BF = 0, 1
 SLOT_BYTES = AT_WB_BF + PACK * N * 2
 GATHERS = ((0, 4), (4, 8), (8, 9), (9, 10), (10, 11), (11, 12))
 LATE_GATHER_LEAD = 4
-LAST_CUT = 44
-W_LOADS = ((0, 4), (4, 8), (8, 12))
+SCALAR_COLS = 448
+LAST_SCALAR_COLS = 176
+W_LOADS = ((0, 4), (4, 8), (8, 10), (10, 12))
 STORES = ((0, 8), (8, 10), (10, 12))
 PLANE_EXPERTS = 3
 
@@ -90,8 +91,9 @@ def tile_moe_elr_s_gelu_kernel(
             else:
                 load_wa(e)
                 load_wb(e)
-            if span_of(W_LOADS, e)[0] == e:
-                load_w(span_of(W_LOADS, e))
+            span = span_of(W_LOADS, e)
+            if e == (span[0] if span[1] < E else E - 1):
+                load_w(span)
 
         nc.sync.dma_start(offsets[:], offs)
         nc.sync.dma_start(
@@ -149,13 +151,11 @@ def tile_moe_elr_s_gelu_kernel(
 
         def cast_wb(e):
             wb_bf[e] = in_slot(e, [P, PACK * N], BF16, "wb_bf", AT_WB_BF)
-            grouped = wb_bf[e][:].rearrange("p (c i j) -> p c j i", i=4, j=PACK)
-            rows = wb_raw[e][:].rearrange("p j (c i) -> p c j i", i=4)
-            if e < E - 1:
-                nc.scalar.copy(out=grouped, in_=rows)
-            else:
-                nc.scalar.copy(out=grouped[:, :LAST_CUT], in_=rows[:, :LAST_CUT])
-                nc.vector.tensor_copy(out=grouped[:, LAST_CUT:], in_=rows[:, LAST_CUT:])
+            grouped = wb_bf[e][:].rearrange("p (c i j) -> p c j i", i=2, j=PACK)
+            rows = wb_raw[e][:].rearrange("p j (c i) -> p c j i", i=2)
+            cut = (SCALAR_COLS if e < E - 1 else LAST_SCALAR_COLS) // 2
+            nc.scalar.copy(out=grouped[:, :cut], in_=rows[:, :cut])
+            nc.vector.tensor_copy(out=grouped[:, cut:], in_=rows[:, cut:])
 
         def quantize_wa(e):
             codes = work.tile([P, H], U32, name="wa_codes", align_bytes=64)
@@ -248,8 +248,8 @@ def tile_moe_elr_s_gelu_kernel(
             span, cols = store_cols(e)
             y_bf[e] = in_slot(e + 3, [P, C * PACK], BF16, "y_bf", AT_Y_BF)
             nc.vector.tensor_copy(
-                out=y_bf[e][:].rearrange("p (c i t) -> p c t i", i=4, t=PACK),
-                in_=y_f32[span][:, :, cols].rearrange("p t (c i) -> p c t i", i=4),
+                out=y_bf[e][:].rearrange("p (c i t) -> p c t i", i=2, t=PACK),
+                in_=y_f32[span][:, :, cols].rearrange("p t (c i) -> p c t i", i=2),
             )
 
         def quantize_y(e):
@@ -291,8 +291,11 @@ def tile_moe_elr_s_gelu_kernel(
             (late_gather, -LATE_GATHER_LEAD),
         )
         for step in range(E + 3):
+            first = (cast_wa, quantize_wa, first_product) if step == E - 1 else ()
+            for stage in first:
+                stage(step)
             for stage, lag in stages:
-                if 0 <= step - lag < E:
+                if 0 <= step - lag < E and stage not in first:
                     stage(step - lag)
             if 1 <= step and step - 1 + SLOTS < E:
                 load_expert(step - 1 + SLOTS)

@@ -22,11 +22,11 @@ QUADS = 4
 QUAD = 32
 LIST_COLS = C // 16
 SLOTS = 8
-AT_H_BF, AT_Y_DEALT, AT_Y_BF, AT_WB_SCALES, AT_WORDS, AT_SCALES, AT_WB_BF = 0, 1024, 3072, 4096, 4608, 5120, 5248
+AT_H_BF, AT_Y_DEALT, AT_Y_BF, AT_WB_SCALES, AT_WORDS, AT_SCALES, AT_WB_BF = 0, 1024, 3072, 4096, 4608, 5120, 5376
 SLOT_BYTES = AT_WB_BF + PACK * N * 2
 GATHERS = ((0, 4), (4, 8), (8, 9), (9, 10), (10, 11), (11, 12))
 LATE_GATHER_LEAD = 4
-SCALAR_COLS = 448
+SCALAR_Y_CASTS = 8
 LAST_SCALAR_COLS = 176
 W_LOADS = ((0, 4), (4, 8), (8, 10), (10, 12))
 STORES = ((0, 8), (8, 10), (10, 12))
@@ -50,11 +50,11 @@ def tile_moe_elr_s_gelu_kernel(
         psum_y = ctx.enter_context(tc.psum_pool(name="psum_y", bufs=3))
 
         offsets = keep.tile([P, E * LIST_COLS], U16, name="offsets")
-        tok_words = keep.tile([P, T], U32, name="tok_words", align_bytes=64)
-        tok_scales = keep.tile([P, T], U8, name="tok_scales", align_bytes=64)
-        w_planes = keep.tile([P, E, N], U8, name="w_planes", align_bytes=64)
+        tok_words = keep.tile([P, T], U32, name="tok_words", align_bytes=256)
+        tok_scales = keep.tile([P, T], U8, name="tok_scales", align_bytes=256)
+        w_planes = keep.tile([P, E, N], U8, name="w_planes", align_bytes=256)
         ident = keep.tile([P, P], F32, name="ident")
-        y_planes = keep.tile([P, PLANE_EXPERTS * C], U8, name="y_planes", align_bytes=64)
+        y_planes = keep.tile([P, PLANE_EXPERTS * C], U8, name="y_planes", align_bytes=256)
 
         nc.gpsimd.memset(tok_scales[:].bitcast(I32), 0)
         nc.vector.memset(w_planes[:].bitcast(I32), 0)
@@ -65,7 +65,7 @@ def tile_moe_elr_s_gelu_kernel(
         def in_slot(e, shape, dtype, name, at):
             slot = e % SLOTS
             return ring.tile(
-                shape, dtype, name="%s_%d" % (name, slot), align_bytes=64, offset=slot * SLOT_BYTES + at
+                shape, dtype, name="%s_%d" % (name, slot), align_bytes=256, offset=slot * SLOT_BYTES + at
             )
 
         def load_wa(e):
@@ -73,12 +73,12 @@ def tile_moe_elr_s_gelu_kernel(
             nc.sync.dma_start(out=wa_raw[e][:], in_=wa[e].rearrange("(p j) i -> p j i", j=PACK))
 
         def load_wb(e):
-            wb_raw[e] = wb_pool.tile([P, PACK, N], F32, name="wb_raw")
+            wb_raw[e] = wb_pool.tile([P, PACK, N], F32, name="wb_raw", align_bytes=256)
             nc.sync.dma_start(out=wb_raw[e][:], in_=wb[e].rearrange("(p j) n -> p j n", j=PACK))
 
         def load_w(span):
             first, last = span
-            w_codes[span] = keep.tile([P, last - first, 2 * N], U8, name="w_codes_%d" % first, align_bytes=64)
+            w_codes[span] = keep.tile([P, last - first, 2 * N], U8, name="w_codes_%d" % first, align_bytes=256)
             nc.sync.dma_start(
                 out=w_codes[span][:].bitcast(I32),
                 in_=w_words[first:last, 0].rearrange("e p b -> p e b").bitcast(I32),
@@ -153,9 +153,12 @@ def tile_moe_elr_s_gelu_kernel(
             wb_bf[e] = in_slot(e, [P, PACK * N], BF16, "wb_bf", AT_WB_BF)
             grouped = wb_bf[e][:].rearrange("p (c i j) -> p c j i", i=2, j=PACK)
             rows = wb_raw[e][:].rearrange("p j (c i) -> p c j i", i=2)
-            cut = (SCALAR_COLS if e < E - 1 else LAST_SCALAR_COLS) // 2
-            nc.scalar.copy(out=grouped[:, :cut], in_=rows[:, :cut])
-            nc.vector.tensor_copy(out=grouped[:, cut:], in_=rows[:, cut:])
+            if e < E - 1:
+                nc.scalar.copy(out=grouped, in_=rows)
+            else:
+                cut = LAST_SCALAR_COLS // 2
+                nc.scalar.copy(out=grouped[:, :cut], in_=rows[:, :cut])
+                nc.vector.tensor_copy(out=grouped[:, cut:], in_=rows[:, cut:])
 
         def quantize_wa(e):
             codes = work.tile([P, H], U32, name="wa_codes", align_bytes=64)
@@ -219,7 +222,7 @@ def tile_moe_elr_s_gelu_kernel(
                 stop=True,
             )
 
-        def turn(e):
+        def deal(e):
             y_dealt = in_slot(e + 2, [C, PACK, P], F32, "y_dealt", AT_Y_DEALT)
             nc.scalar.copy(out=y_dealt[:], in_=y_rows[e][:].rearrange("u (m t) -> u t m", t=PACK))
             y_cols[e] = psum_y.tile([P, PACK, C], F32, name="y_cols")
@@ -235,8 +238,8 @@ def tile_moe_elr_s_gelu_kernel(
             first, last = span
             if e == first:
                 width = (last - first) * C
-                y_f32[span] = keep.tile([P, PACK, width], F32, name="y_f32_%d" % first)
-                y_codes[span] = keep.tile([P, width], U32, name="y_codes_%d" % first, align_bytes=64)
+                y_f32[span] = keep.tile([P, PACK, width], F32, name="y_f32_%d" % first, align_bytes=256)
+                y_codes[span] = keep.tile([P, width], U32, name="y_codes_%d" % first, align_bytes=256)
             nc.scalar.copy(out=y_f32[span][:, :, cols], in_=y_cols[e][:])
             if e == last - 1:
                 nc.sync.dma_start(
@@ -247,7 +250,8 @@ def tile_moe_elr_s_gelu_kernel(
         def cast_y(e):
             span, cols = store_cols(e)
             y_bf[e] = in_slot(e + 3, [P, C * PACK], BF16, "y_bf", AT_Y_BF)
-            nc.vector.tensor_copy(
+            copy = nc.scalar.copy if e < SCALAR_Y_CASTS else nc.vector.tensor_copy
+            copy(
                 out=y_bf[e][:].rearrange("p (c i t) -> p c t i", i=2, t=PACK),
                 in_=y_f32[span][:, :, cols].rearrange("p t (c i) -> p c t i", i=2),
             )
@@ -278,11 +282,11 @@ def tile_moe_elr_s_gelu_kernel(
         stages = (
             (cast_wa, 0),
             (gelu, 1),
-            (turn, 2),
-            (cast_wb, 0),
-            (empty, 2),
+            (deal, 2),
             (quantize_wb, 1),
             (cast_y, 3),
+            (cast_wb, 0),
+            (empty, 2),
             (quantize_h, 1),
             (second_product, 1),
             (quantize_wa, 0),

@@ -26,7 +26,7 @@ AT_H_BF, AT_Y_DEALT, AT_Y_BF, AT_WB_SCALES, AT_WORDS, AT_SCALES, AT_WB_BF = 0, 1
 SLOT_BYTES = AT_WB_BF + PACK * N * 2
 GATHERS = ((0, 4), (4, 8), (8, 9), (9, 10), (10, 11), (11, 12))
 LATE_GATHER_LEAD = 4
-SCALAR_Y_CASTS = 8
+Y_CAST_LAG = 3
 LAST_SCALAR_COLS = 176
 W_LOADS = ((0, 4), (4, 8), (8, 10), (10, 12))
 STORES = ((0, 8), (8, 10), (10, 12))
@@ -99,16 +99,16 @@ def tile_moe_elr_s_gelu_kernel(
         nc.sync.dma_start(
             out=tok_words[:].bitcast(I32), in_=x_words[0].rearrange("p t d -> p (t d)").bitcast(I32)
         )
-        for q in range(QUADS):
+        for r in range(4):
             nc.scalar.dma_start(
-                out=tok_scales[QUAD * q : QUAD * q + 4, :].bitcast(I32),
-                in_=x_scales[0, 4 * q : 4 * q + 4, :].bitcast(I32),
+                out=tok_scales[r:P:QUAD, :].bitcast(I32),
+                in_=x_scales[0].rearrange("(q r) t -> r q t", r=4)[r].bitcast(I32),
             )
         load_expert(0)
-        for q in range(QUADS):
+        for r in range(4):
             nc.sync.dma_start(
-                out=w_planes[QUAD * q : QUAD * q + 4].bitcast(I32),
-                in_=w_scales[:, 0, 4 * q : 4 * q + 4, :].rearrange("e r n -> r e n").bitcast(I32),
+                out=w_planes[r:P:QUAD].bitcast(I32),
+                in_=w_scales[:, 0].rearrange("e (q r) n -> r q e n", r=4)[r].bitcast(I32),
             )
         for e in range(1, SLOTS):
             load_expert(e)
@@ -250,7 +250,8 @@ def tile_moe_elr_s_gelu_kernel(
         def cast_y(e):
             span, cols = store_cols(e)
             y_bf[e] = in_slot(e + 3, [P, C * PACK], BF16, "y_bf", AT_Y_BF)
-            copy = nc.scalar.copy if e < SCALAR_Y_CASTS else nc.vector.tensor_copy
+            vector_gathers = SLOTS <= e + Y_CAST_LAG + LATE_GATHER_LEAD < E
+            copy = nc.scalar.copy if vector_gathers else nc.vector.tensor_copy
             copy(
                 out=y_bf[e][:].rearrange("p (c i t) -> p c t i", i=2, t=PACK),
                 in_=y_f32[span][:, :, cols].rearrange("p t (c i) -> p c t i", i=2),
@@ -284,7 +285,7 @@ def tile_moe_elr_s_gelu_kernel(
             (gelu, 1),
             (deal, 2),
             (quantize_wb, 1),
-            (cast_y, 3),
+            (cast_y, Y_CAST_LAG),
             (cast_wb, 0),
             (empty, 2),
             (quantize_h, 1),

@@ -145,18 +145,18 @@ def tile_moe_elr_s_gelu_kernel(
         def cast_wa(e):
             wa_bf[e] = work.tile([P, PACK * H], BF16, name="wa_bf", align_bytes=64)
             nc.vector.tensor_copy(
-                out=wa_bf[e][:].rearrange("p (t m j) -> p m t j", t=PACK, j=PACK),
-                in_=wa_raw[e][:].rearrange("p j (m t) -> p m t j", t=PACK),
+                out=wa_bf[e][:].rearrange("p (t m j) -> p m j t", t=PACK, j=PACK),
+                in_=wa_raw[e][:].rearrange("p j (m t) -> p m j t", t=PACK),
             )
 
         def cast_wb(e):
             wb_bf[e] = in_slot(e, [P, PACK * N], BF16, "wb_bf", AT_WB_BF)
-            grouped = wb_bf[e][:].rearrange("p (c i j) -> p c j i", i=2, j=PACK)
-            rows = wb_raw[e][:].rearrange("p j (c i) -> p c j i", i=2)
+            grouped = wb_bf[e][:].rearrange("p (c i j) -> p c j i", i=4, j=PACK)
+            rows = wb_raw[e][:].rearrange("p j (c i) -> p c j i", i=4)
             if e < E - 1:
                 nc.scalar.copy(out=grouped, in_=rows)
             else:
-                cut = LAST_SCALAR_COLS // 2
+                cut = LAST_SCALAR_COLS // 4
                 nc.scalar.copy(out=grouped[:, :cut], in_=rows[:, :cut])
                 nc.vector.tensor_copy(out=grouped[:, cut:], in_=rows[:, cut:])
 
@@ -253,8 +253,8 @@ def tile_moe_elr_s_gelu_kernel(
             vector_gathers = SLOTS <= e + Y_CAST_LAG + LATE_GATHER_LEAD < E
             copy = nc.scalar.copy if vector_gathers else nc.vector.tensor_copy
             copy(
-                out=y_bf[e][:].rearrange("p (c i t) -> p c t i", i=2, t=PACK),
-                in_=y_f32[span][:, :, cols].rearrange("p t (c i) -> p c t i", i=2),
+                out=y_bf[e][:].rearrange("p (c i t) -> p c t i", i=4, t=PACK),
+                in_=y_f32[span][:, :, cols].rearrange("p t (c i) -> p c t i", i=4),
             )
 
         def quantize_y(e):

@@ -21,14 +21,15 @@ PACK = 4
 QUADS = 4
 QUAD = 32
 LIST_COLS = C // 16
-SLOTS = 8
-AT_H_BF, AT_Y_DEALT, AT_Y_BF, AT_WB_SCALES, AT_WORDS, AT_SCALES, AT_WB_BF = 0, 1024, 3072, 4096, 4608, 5120, 5376
-SLOT_BYTES = AT_WB_BF + PACK * N * 2
-GATHERS = ((0, 4), (4, 8), (8, 9), (9, 10), (10, 11), (11, 12))
-LATE_GATHER_LEAD = 4
-Y_CAST_LAG = 3
-LAST_SCALAR_COLS = 176
-W_LOADS = ((0, 4), (4, 8), (8, 10), (10, 12))
+LAST = E - 1
+WA_SLOTS, WB_SLOTS = 10, 8
+FIRST_REUSED = 2
+SLOT_BYTES = PACK * H * 4
+AT_H_CODES, AT_WB_SCALES, AT_Y_BF, AT_WORDS, AT_SCALES = 0, 512, 1024, 2048, 4096
+AT_H_BF, AT_Y_DEALT = 0, 1024
+GATHER = 4
+VECTOR_COLS = 64
+W_LOADS = ((0, 4), (4, 8), (8, 12))
 STORES = ((0, 8), (8, 10), (10, 12))
 PLANE_EXPERTS = 3
 
@@ -43,11 +44,10 @@ def tile_moe_elr_s_gelu_kernel(
     nc = tc.nc
     with ExitStack() as ctx:
         keep = ctx.enter_context(tc.tile_pool(name="keep", bufs=1))
-        ring = ctx.enter_context(tc.tile_pool(name="ring", bufs=1))
-        wb_pool = ctx.enter_context(tc.tile_pool(name="wb_pool", bufs=SLOTS))
-        work = ctx.enter_context(tc.tile_pool(name="work", bufs=3))
-        psum_h = ctx.enter_context(tc.psum_pool(name="psum_h", bufs=2))
-        psum_y = ctx.enter_context(tc.psum_pool(name="psum_y", bufs=3))
+        wa_ring = ctx.enter_context(tc.tile_pool(name="wa_ring", bufs=1))
+        wb_ring = ctx.enter_context(tc.tile_pool(name="wb_ring", bufs=1))
+        work = ctx.enter_context(tc.tile_pool(name="work", bufs=2))
+        psum = ctx.enter_context(tc.psum_pool(name="psum", bufs=2))
 
         offsets = keep.tile([P, E * LIST_COLS], U16, name="offsets")
         tok_words = keep.tile([P, T], U32, name="tok_words", align_bytes=256)
@@ -62,19 +62,14 @@ def tile_moe_elr_s_gelu_kernel(
 
         wa_raw, wb_raw, w_codes = {}, {}, {}
 
-        def in_slot(e, shape, dtype, name, at):
-            slot = e % SLOTS
+        def in_slot(ring, e, shape, dtype, name, at):
+            if ring is wa_ring:
+                slot = e if e < WA_SLOTS else e - WA_SLOTS + FIRST_REUSED
+            else:
+                slot = e % WB_SLOTS
             return ring.tile(
                 shape, dtype, name="%s_%d" % (name, slot), align_bytes=256, offset=slot * SLOT_BYTES + at
             )
-
-        def load_wa(e):
-            wa_raw[e] = in_slot(e, [P, PACK, H], F32, "wa_raw", 0)
-            nc.sync.dma_start(out=wa_raw[e][:], in_=wa[e].rearrange("(p j) i -> p j i", j=PACK))
-
-        def load_wb(e):
-            wb_raw[e] = wb_pool.tile([P, PACK, N], F32, name="wb_raw", align_bytes=256)
-            nc.sync.dma_start(out=wb_raw[e][:], in_=wb[e].rearrange("(p j) n -> p j n", j=PACK))
 
         def load_w(span):
             first, last = span
@@ -85,22 +80,30 @@ def tile_moe_elr_s_gelu_kernel(
             )
 
         def load_expert(e):
-            if e < E - 1:
-                load_wb(e)
-                load_wa(e)
+            wa_raw[e] = in_slot(wa_ring, e, [P, PACK, H], F32, "wa_raw", 0)
+            nc.sync.dma_start(out=wa_raw[e][:], in_=wa[e].rearrange("(p j) i -> p j i", j=PACK))
+            rows = wb[e].rearrange("(p j) n -> p j n", j=PACK)
+            if e < LAST:
+                wb_raw[e] = in_slot(wb_ring, e, [P, PACK, N], F32, "wb_raw", 0)
+                nc.sync.dma_start(out=wb_raw[e][:], in_=rows)
             else:
-                load_wa(e)
-                load_wb(e)
-            span = span_of(W_LOADS, e)
-            if e == (span[0] if span[1] < E else E - 1):
-                load_w(span)
+                wb_raw[e] = []
+                for half in range(2):
+                    part = in_slot(
+                        wb_ring, e, [P, PACK, N // 2], F32, "wb_half_%d" % half, half * SLOT_BYTES // 2
+                    )
+                    nc.sync.dma_start(out=part[:], in_=rows[:, :, half * N // 2 : (half + 1) * N // 2])
+                    wb_raw[e].append(part)
+            for span in W_LOADS:
+                if e == max(span[0] - 1, 0):
+                    load_w(span)
 
         nc.sync.dma_start(offsets[:], offs)
         nc.sync.dma_start(
             out=tok_words[:].bitcast(I32), in_=x_words[0].rearrange("p t d -> p (t d)").bitcast(I32)
         )
         for r in range(4):
-            nc.scalar.dma_start(
+            nc.sync.dma_start(
                 out=tok_scales[r:P:QUAD, :].bitcast(I32),
                 in_=x_scales[0].rearrange("(q r) t -> r q t", r=4)[r].bitcast(I32),
             )
@@ -110,55 +113,73 @@ def tile_moe_elr_s_gelu_kernel(
                 out=w_planes[r:P:QUAD].bitcast(I32),
                 in_=w_scales[:, 0].rearrange("e (q r) n -> r q e n", r=4)[r].bitcast(I32),
             )
-        for e in range(1, SLOTS):
+        for e in range(1, WB_SLOTS):
             load_expert(e)
 
         slot_words, slot_scales = {}, {}
 
-        def gather(span):
-            first, last = span
-            width = (last - first) * C
+        def gather(first, last, words, scales):
             picks = offsets[:, first * LIST_COLS : last * LIST_COLS]
-            if first < SLOTS:
-                slot_words[span] = keep.tile([P, width], U32, name="slot_words_%d" % first, align_bytes=64)
-                slot_scales[span] = keep.tile([P, width], U8, name="slot_scales_%d" % first, align_bytes=64)
-            else:
-                slot_words[span] = in_slot(first - LATE_GATHER_LEAD, [P, width], U32, "slot_words", AT_WORDS)
-                slot_scales[span] = in_slot(first - LATE_GATHER_LEAD, [P, width], U8, "slot_scales", AT_SCALES)
-            nc.vector.tensor_copy(slot_words[span][:], tok_words[:].indirect(picks))
-            nc.vector.tensor_copy(slot_scales[span][:], tok_scales[:].indirect(picks))
+            nc.vector.tensor_copy(words[:], tok_words[:].indirect(picks))
+            nc.vector.tensor_copy(scales[:], tok_scales[:].indirect(picks))
+            for e in range(first, last):
+                cols = slice((e - first) * C, (e - first + 1) * C)
+                slot_words[e], slot_scales[e] = words[:, cols].bitcast(FP8X4), scales[:, cols]
 
-        def slots_of(e):
-            span = span_of(GATHERS, e)
-            cols = slice((e - span[0]) * C, (e - span[0] + 1) * C)
-            return slot_words[span][:, cols].bitcast(FP8X4), slot_scales[span][:, cols]
+        def late_gather(e):
+            first = (e + 1) * GATHER
+            if first < E:
+                words = in_slot(wa_ring, e, [P, GATHER * C], U32, "slot_words", AT_WORDS)
+                scales = in_slot(wa_ring, e, [P, GATHER * C], U8, "slot_scales", AT_SCALES)
+                gather(first, first + GATHER, words, scales)
 
         wa_bf, wb_bf, h_bf, y_bf = {}, {}, {}, {}
         wa_q, wb_q, h_q = {}, {}, {}
         pre, y_rows, y_cols = {}, {}, {}
         y_f32, y_codes = {}, {}
+        w_dealt = {}
 
         def quantize(values, codes, scales):
             nc.vector.quantize_mx(out=codes[:].bitcast(FP8X4), scales=scales[:], in_=values[:])
             return codes, scales
 
+        def dealt(values):
+            return values[:].rearrange("p (t m j) -> p m j t", t=PACK, j=PACK)
+
         def cast_wa(e):
             wa_bf[e] = work.tile([P, PACK * H], BF16, name="wa_bf", align_bytes=64)
             nc.vector.tensor_copy(
-                out=wa_bf[e][:].rearrange("p (t m j) -> p m j t", t=PACK, j=PACK),
-                in_=wa_raw[e][:].rearrange("p j (m t) -> p m j t", t=PACK),
+                out=dealt(wa_bf[e]), in_=wa_raw[e][:].rearrange("p j (m t) -> p m j t", t=PACK)
             )
 
         def cast_wb(e):
-            wb_bf[e] = in_slot(e, [P, PACK * N], BF16, "wb_bf", AT_WB_BF)
-            grouped = wb_bf[e][:].rearrange("p (c i j) -> p c j i", i=4, j=PACK)
-            rows = wb_raw[e][:].rearrange("p j (c i) -> p c j i", i=4)
-            if e < E - 1:
-                nc.scalar.copy(out=grouped, in_=rows)
+            wb_bf[e] = work.tile([P, PACK * N], BF16, name="wb_bf", align_bytes=64)
+            if e < LAST:
+                grouped = wb_bf[e][:].rearrange("p (c i j) -> p c j i", i=4, j=PACK)
+                rows = wb_raw[e][:].rearrange("p j (c i) -> p c j i", i=4)
+                cut = VECTOR_COLS // 4
+                nc.vector.tensor_copy(out=grouped[:, :cut], in_=rows[:, :cut])
+                nc.scalar.copy(out=grouped[:, cut:], in_=rows[:, cut:])
             else:
-                cut = LAST_SCALAR_COLS // 4
-                nc.scalar.copy(out=grouped[:, :cut], in_=rows[:, :cut])
-                nc.vector.tensor_copy(out=grouped[:, cut:], in_=rows[:, cut:])
+                for half, copy in enumerate((nc.scalar.copy, nc.vector.tensor_copy)):
+                    copy(
+                        out=dealt(wb_bf[e])[:, half * P // 2 : (half + 1) * P // 2],
+                        in_=wb_raw[e][half][:].rearrange("p j (m t) -> p m j t", t=PACK),
+                    )
+
+        def deal_last_w():
+            span = span_of(W_LOADS, LAST)
+            words = keep.tile([P, 2 * N], U8, name="w_dealt_words", align_bytes=64)
+            scales = keep.tile([P, N], U8, name="w_dealt_scales", align_bytes=64)
+            nc.vector.tensor_copy(
+                out=words[:].bitcast(U16).rearrange("p (t m) -> p t m", t=PACK),
+                in_=w_codes[span][:, LAST - span[0], :].bitcast(U16).rearrange("p (m t) -> p t m", t=PACK),
+            )
+            nc.vector.tensor_copy(
+                out=scales[:].rearrange("p (t m) -> p t m", t=PACK),
+                in_=w_planes[:, LAST, :].rearrange("p (m t) -> p t m", t=PACK),
+            )
+            w_dealt[LAST] = words, scales
 
         def quantize_wa(e):
             codes = work.tile([P, H], U32, name="wa_codes", align_bytes=64)
@@ -167,32 +188,31 @@ def tile_moe_elr_s_gelu_kernel(
 
         def quantize_wb(e):
             codes = work.tile([P, N], U32, name="wb_codes", align_bytes=64)
-            scales = in_slot(e + 1, [P, N], U8, "wb_scales", AT_WB_SCALES)
+            scales = in_slot(wa_ring, e + 1, [P, N], U8, "wb_scales", AT_WB_SCALES)
             wb_q[e] = quantize(wb_bf[e], codes, scales)
 
         def quantize_h(e):
-            codes = work.tile([P, C], U32, name="h_codes", align_bytes=64)
+            codes = in_slot(wa_ring, e + 1, [P, C], U32, "h_codes", AT_H_CODES)
             scales = work.tile([P, C], U8, name="h_scales", align_bytes=64)
             h_q[e] = quantize(h_bf[e], codes, scales)
 
         def first_product(e):
-            x_codes, x_plane = slots_of(e)
             codes, scales = wa_q[e]
-            pre[e] = psum_h.tile([P, PACK, C], F32, name="pre")
+            pre[e] = psum.tile([P, PACK, C], F32, name="pre")
             for t in range(PACK):
                 cols = slice(t * P, (t + 1) * P)
                 nc.tensor.matmul_mx(
                     out=pre[e][:, t, :],
                     lhsT=codes[:, cols].bitcast(FP8X4),
                     lhsT_scale=scales[:, cols],
-                    rhs=x_codes,
-                    rhs_scale=x_plane,
+                    rhs=slot_words[e],
+                    rhs_scale=slot_scales[e],
                     start=True,
                     stop=True,
                 )
 
         def gelu(e):
-            h_bf[e] = in_slot(e + 1, [P, C * PACK], BF16, "h_bf", AT_H_BF)
+            h_bf[e] = in_slot(wb_ring, e, [P, C * PACK], BF16, "h_bf", AT_H_BF)
             nc.scalar.activation(
                 out=h_bf[e][:].rearrange("p (u t) -> p u t", t=PACK),
                 in_=pre[e][:].rearrange("p t u -> p u t"),
@@ -200,13 +220,14 @@ def tile_moe_elr_s_gelu_kernel(
             )
 
         def second_product(e):
-            x_codes, x_plane = slots_of(e)
+            if e == LAST:
+                return last_product()
             w_span = span_of(W_LOADS, e)
-            y_rows[e] = psum_y.tile([C, N], F32, name="y_rows")
+            y_rows[e] = psum.tile([C, N], F32, name="y_rows")
             nc.tensor.matmul_mx(
                 out=y_rows[e][:],
-                lhsT=x_codes,
-                lhsT_scale=x_plane,
+                lhsT=slot_words[e],
+                lhsT_scale=slot_scales[e],
                 rhs=w_codes[w_span][:, e - w_span[0], :].bitcast(FP4X4),
                 rhs_scale=w_planes[:, e, :],
                 start=True,
@@ -222,10 +243,38 @@ def tile_moe_elr_s_gelu_kernel(
                 stop=True,
             )
 
+        def last_product():
+            words, scales = w_dealt[LAST]
+            y_cols[LAST] = psum.tile([P, PACK, C], F32, name="y_cols")
+            for t in range(PACK):
+                cols = slice(t * P, (t + 1) * P)
+                nc.tensor.matmul_mx(
+                    out=y_cols[LAST][:, t, :],
+                    lhsT=words[:, 2 * t * P : 2 * (t + 1) * P].bitcast(FP4X4),
+                    lhsT_scale=scales[:, cols],
+                    rhs=slot_words[LAST],
+                    rhs_scale=slot_scales[LAST],
+                    start=True,
+                    stop=False,
+                )
+                nc.tensor.matmul_mx(
+                    out=y_cols[LAST][:, t, :],
+                    lhsT=wb_q[LAST][0][:, cols].bitcast(FP8X4),
+                    lhsT_scale=wb_q[LAST][1][:, cols],
+                    rhs=h_q[LAST][0][:].bitcast(FP8X4),
+                    rhs_scale=h_q[LAST][1][:],
+                    start=False,
+                    stop=True,
+                )
+
         def deal(e):
-            y_dealt = in_slot(e + 2, [C, PACK, P], F32, "y_dealt", AT_Y_DEALT)
-            nc.scalar.copy(out=y_dealt[:], in_=y_rows[e][:].rearrange("u (m t) -> u t m", t=PACK))
-            y_cols[e] = psum_y.tile([P, PACK, C], F32, name="y_cols")
+            if e == LAST:
+                return
+            y_dealt = in_slot(wb_ring, e + 1, [C, PACK, P], F32, "y_dealt", AT_Y_DEALT)
+            by_t = y_rows[e][:].rearrange("u (m t) -> u t m", t=PACK)
+            for t in range(0, PACK, 2):
+                nc.scalar.copy(out=y_dealt[:, t : t + 2, :], in_=by_t[:, t : t + 2, :])
+            y_cols[e] = psum.tile([P, PACK, C], F32, name="y_cols")
             for t in range(PACK):
                 nc.tensor.transpose(y_cols[e][:, t, :], y_dealt[:, t, :], ident[:])
 
@@ -249,10 +298,8 @@ def tile_moe_elr_s_gelu_kernel(
 
         def cast_y(e):
             span, cols = store_cols(e)
-            y_bf[e] = in_slot(e + 3, [P, C * PACK], BF16, "y_bf", AT_Y_BF)
-            vector_gathers = SLOTS <= e + Y_CAST_LAG + LATE_GATHER_LEAD < E
-            copy = nc.scalar.copy if vector_gathers else nc.vector.tensor_copy
-            copy(
+            y_bf[e] = in_slot(wa_ring, e + 2, [P, C * PACK], BF16, "y_bf", AT_Y_BF)
+            nc.vector.tensor_copy(
                 out=y_bf[e][:].rearrange("p (c i t) -> p c t i", i=4, t=PACK),
                 in_=y_f32[span][:, :, cols].rearrange("p t (c i) -> p c t i", i=4),
             )
@@ -272,38 +319,37 @@ def tile_moe_elr_s_gelu_kernel(
                     in_=y_codes[span][:].bitcast(I32),
                 )
 
-        def late_gather(e):
-            if e >= SLOTS:
-                gather(span_of(GATHERS, e))
-
-        for span in GATHERS:
-            if span[0] < SLOTS:
-                gather(span)
+        gather(
+            0,
+            GATHER,
+            keep.tile([P, GATHER * C], U32, name="first_words", align_bytes=64),
+            keep.tile([P, GATHER * C], U8, name="first_scales", align_bytes=64),
+        )
 
         stages = (
             (cast_wa, 0),
-            (gelu, 1),
-            (deal, 2),
-            (quantize_wb, 1),
-            (cast_y, Y_CAST_LAG),
-            (cast_wb, 0),
-            (empty, 2),
             (quantize_h, 1),
-            (second_product, 1),
             (quantize_wa, 0),
             (first_product, 0),
-            (quantize_y, 3),
-            (late_gather, -LATE_GATHER_LEAD),
+            (quantize_wb, 1),
+            (second_product, 1),
+            (cast_wb, 0),
+            (cast_y, 2),
+            (late_gather, 0),
+            (quantize_y, 2),
+            (deal, 1),
+            (gelu, 0),
+            (empty, 1),
         )
-        for step in range(E + 3):
-            first = (cast_wa, quantize_wa, first_product) if step == E - 1 else ()
-            for stage in first:
-                stage(step)
+        for step in range(E + 2):
             for stage, lag in stages:
-                if 0 <= step - lag < E and stage not in first:
+                if 0 <= step - lag < E:
                     stage(step - lag)
-            if 1 <= step and step - 1 + SLOTS < E:
-                load_expert(step - 1 + SLOTS)
+            reload = step - 1 + WB_SLOTS
+            if WB_SLOTS <= reload < E:
+                load_expert(reload)
+            if step == W_LOADS[-1][0]:
+                deal_last_w()
 
         for q in range(QUADS):
             nc.sync.dma_start(

@@ -48,6 +48,7 @@ def tile_moe_elr_s_gelu_kernel(
         wb_ring = ctx.enter_context(tc.tile_pool(name="wb_ring", bufs=1))
         work = ctx.enter_context(tc.tile_pool(name="work", bufs=2))
         psum = ctx.enter_context(tc.psum_pool(name="psum", bufs=2))
+        last_psum = ctx.enter_context(tc.psum_pool(name="last_psum", bufs=1))
 
         offsets = keep.tile([P, E * LIST_COLS], U16, name="offsets")
         tok_words = keep.tile([P, T], U32, name="tok_words", align_bytes=256)
@@ -245,26 +246,28 @@ def tile_moe_elr_s_gelu_kernel(
 
         def last_product():
             words, scales = w_dealt[LAST]
-            y_cols[LAST] = psum.tile([P, PACK, C], F32, name="y_cols")
+            y_cols[LAST] = [last_psum.tile([P, 2, C], F32, name="y_last_%d" % half) for half in range(2)]
             for t in range(PACK):
                 cols = slice(t * P, (t + 1) * P)
                 nc.tensor.matmul_mx(
-                    out=y_cols[LAST][:, t, :],
+                    out=y_cols[LAST][t // 2][:, t % 2, :],
                     lhsT=words[:, 2 * t * P : 2 * (t + 1) * P].bitcast(FP4X4),
                     lhsT_scale=scales[:, cols],
                     rhs=slot_words[LAST],
                     rhs_scale=slot_scales[LAST],
-                    start=True,
+                    start=t % 2 == 0,
                     stop=False,
                 )
+            for t in range(PACK):
+                cols = slice(t * P, (t + 1) * P)
                 nc.tensor.matmul_mx(
-                    out=y_cols[LAST][:, t, :],
+                    out=y_cols[LAST][t // 2][:, t % 2, :],
                     lhsT=wb_q[LAST][0][:, cols].bitcast(FP8X4),
                     lhsT_scale=wb_q[LAST][1][:, cols],
                     rhs=h_q[LAST][0][:].bitcast(FP8X4),
                     rhs_scale=h_q[LAST][1][:],
                     start=False,
-                    stop=True,
+                    stop=t % 2 == 1,
                 )
 
         def deal(e):
@@ -289,7 +292,11 @@ def tile_moe_elr_s_gelu_kernel(
                 width = (last - first) * C
                 y_f32[span] = keep.tile([P, PACK, width], F32, name="y_f32_%d" % first, align_bytes=256)
                 y_codes[span] = keep.tile([P, width], U32, name="y_codes_%d" % first, align_bytes=256)
-            nc.scalar.copy(out=y_f32[span][:, :, cols], in_=y_cols[e][:])
+            if e < LAST:
+                nc.scalar.copy(out=y_f32[span][:, :, cols], in_=y_cols[e][:])
+            else:
+                for half, copy in enumerate((nc.scalar.copy, nc.vector.tensor_copy)):
+                    copy(out=y_f32[span][:, 2 * half : 2 * half + 2, cols], in_=y_cols[e][half][:])
             if e == last - 1:
                 nc.sync.dma_start(
                     out=out_0.rearrange("(p t) j -> p t j", t=PACK)[:, :, first * C : last * C],
@@ -341,15 +348,39 @@ def tile_moe_elr_s_gelu_kernel(
             (gelu, 0),
             (empty, 1),
         )
-        for step in range(E + 2):
+        for step in range(LAST):
             for stage, lag in stages:
-                if 0 <= step - lag < E:
+                if 0 <= step - lag:
                     stage(step - lag)
             reload = step - 1 + WB_SLOTS
             if WB_SLOTS <= reload < E:
                 load_expert(reload)
             if step == W_LOADS[-1][0]:
                 deal_last_w()
+
+        for stage, lag in (
+            (cast_wa, 0),
+            (quantize_h, 1),
+            (quantize_wa, 0),
+            (first_product, 0),
+            (cast_wb, 0),
+            (gelu, 0),
+            (quantize_wb, 1),
+            (second_product, 1),
+            (quantize_wb, 0),
+            (quantize_h, 0),
+            (second_product, 0),
+            (deal, 1),
+            (empty, 1),
+            (cast_y, 2),
+            (quantize_y, 2),
+            (empty, 0),
+            (cast_y, 1),
+            (cast_y, 0),
+            (quantize_y, 1),
+            (quantize_y, 0),
+        ):
+            stage(LAST - lag)
 
         for q in range(QUADS):
             nc.sync.dma_start(

@@ -28,7 +28,7 @@ SLOT_BYTES = PACK * H * 4
 AT_H_CODES, AT_WB_SCALES, AT_Y_BF, AT_WORDS, AT_SCALES = 0, 512, 1024, 2048, 4096
 AT_H_BF, AT_Y_DEALT = 0, 1024
 GATHER = 4
-VECTOR_COLS = 64
+VECTOR_COLS = 128
 W_LOADS = ((0, 4), (4, 8), (8, 12))
 STORES = ((0, 8), (8, 10), (10, 12))
 PLANE_EXPERTS = 3

@@ -59,7 +59,6 @@ def tile_moe_elr_s_gelu_kernel(
 
         nc.gpsimd.memset(tok_scales[:].bitcast(I32), 0)
         nc.vector.memset(w_planes[:].bitcast(I32), 0)
-        make_identity(nc, ident[:])
 
         wa_raw, wb_raw, w_codes = {}, {}, {}
 
@@ -110,10 +109,11 @@ def tile_moe_elr_s_gelu_kernel(
             )
         load_expert(0)
         for r in range(4):
-            nc.sync.dma_start(
+            nc.gpsimd.dma_start(
                 out=w_planes[r:P:QUAD].bitcast(I32),
                 in_=w_scales[:, 0].rearrange("e (q r) n -> r q e n", r=4)[r].bitcast(I32),
             )
+        make_identity(nc, ident[:])
         for e in range(1, WB_SLOTS):
             load_expert(e)
 

@@ -298,10 +298,14 @@ def tile_moe_elr_s_gelu_kernel(
                 for half, copy in enumerate((nc.scalar.copy, nc.vector.tensor_copy)):
                     copy(out=y_f32[span][:, 2 * half : 2 * half + 2, cols], in_=y_cols[e][half][:])
             if e == last - 1:
-                nc.sync.dma_start(
-                    out=out_0.rearrange("(p t) j -> p t j", t=PACK)[:, :, first * C : last * C],
-                    in_=y_f32[span][:],
-                )
+                rows = out_0.rearrange("(p t) j -> p t j", t=PACK)[:, :, first * C : last * C]
+                if first == 0:
+                    for t in range(PACK):
+                        for half in range(2):
+                            part = slice(half * 4 * C, (half + 1) * 4 * C)
+                            nc.sync.dma_start(out=rows[:, t, part], in_=y_f32[span][:, t, part])
+                else:
+                    nc.sync.dma_start(out=rows, in_=y_f32[span][:])
 
         def cast_y(e):
             span, cols = store_cols(e)

@@ -26,6 +26,7 @@ WA_SLOTS, WB_SLOTS = 10, 8
 FIRST_REUSED = 2
 SLOT_BYTES = PACK * H * 4
 AT_H_CODES, AT_WB_SCALES, AT_Y_BF, AT_WORDS, AT_SCALES = 0, 512, 1024, 2048, 4096
+AT_FIRST_SCALES = 4608
 AT_H_BF, AT_Y_DEALT = 0, 1024
 GATHER = 4
 VECTOR_COLS = 128
@@ -79,9 +80,13 @@ def tile_moe_elr_s_gelu_kernel(
                 in_=w_words[first:last, 0].rearrange("e p b -> p e b").bitcast(I32),
             )
 
-        def load_expert(e):
+        def load_wa(e):
             wa_raw[e] = in_slot(wa_ring, e, [P, PACK, H], F32, "wa_raw", 0)
             nc.sync.dma_start(out=wa_raw[e][:], in_=wa[e].rearrange("(p j) i -> p j i", j=PACK))
+
+        def load_expert(e):
+            if e > 0:
+                load_wa(e)
             rows = wb[e].rearrange("(p j) n -> p j n", j=PACK)
             if e < LAST:
                 wb_raw[e] = in_slot(wb_ring, e, [P, PACK, N], F32, "wb_raw", 0)
@@ -102,6 +107,7 @@ def tile_moe_elr_s_gelu_kernel(
         nc.sync.dma_start(
             out=tok_words[:].bitcast(I32), in_=x_words[0].rearrange("p t d -> p (t d)").bitcast(I32)
         )
+        load_wa(0)
         for r in range(4):
             nc.sync.dma_start(
                 out=tok_scales[r:P:QUAD, :].bitcast(I32),
@@ -119,20 +125,27 @@ def tile_moe_elr_s_gelu_kernel(
 
         slot_words, slot_scales = {}, {}
 
-        def gather(first, last, words, scales):
-            picks = offsets[:, first * LIST_COLS : last * LIST_COLS]
+        def gather_words(first, words):
+            picks = offsets[:, first * LIST_COLS : (first + GATHER) * LIST_COLS]
             nc.vector.tensor_copy(words[:], tok_words[:].indirect(picks))
+            for e in range(GATHER):
+                slot_words[first + e] = words[:, e * C : (e + 1) * C].bitcast(FP8X4)
+
+        def gather_scales(first, scales):
+            picks = offsets[:, first * LIST_COLS : (first + GATHER) * LIST_COLS]
             nc.vector.tensor_copy(scales[:], tok_scales[:].indirect(picks))
-            for e in range(first, last):
-                cols = slice((e - first) * C, (e - first + 1) * C)
-                slot_words[e], slot_scales[e] = words[:, cols].bitcast(FP8X4), scales[:, cols]
+            for e in range(GATHER):
+                slot_scales[first + e] = scales[:, e * C : (e + 1) * C]
+
+        def first_scales(e):
+            if e == 0:
+                gather_scales(0, in_slot(wa_ring, 0, [P, GATHER * C], U8, "first_scales", AT_FIRST_SCALES))
 
         def late_gather(e):
             first = (e + 1) * GATHER
             if first < E:
-                words = in_slot(wa_ring, e, [P, GATHER * C], U32, "slot_words", AT_WORDS)
-                scales = in_slot(wa_ring, e, [P, GATHER * C], U8, "slot_scales", AT_SCALES)
-                gather(first, first + GATHER, words, scales)
+                gather_words(first, in_slot(wa_ring, e, [P, GATHER * C], U32, "slot_words", AT_WORDS))
+                gather_scales(first, in_slot(wa_ring, e, [P, GATHER * C], U8, "slot_scales", AT_SCALES))
 
         wa_bf, wb_bf, h_bf, y_bf = {}, {}, {}, {}
         wa_q, wb_q, h_q = {}, {}, {}
@@ -330,15 +343,11 @@ def tile_moe_elr_s_gelu_kernel(
                     in_=y_codes[span][:].bitcast(I32),
                 )
 
-        gather(
-            0,
-            GATHER,
-            keep.tile([P, GATHER * C], U32, name="first_words", align_bytes=64),
-            keep.tile([P, GATHER * C], U8, name="first_scales", align_bytes=64),
-        )
+        gather_words(0, keep.tile([P, GATHER * C], U32, name="first_words", align_bytes=64))
 
         stages = (
             (cast_wa, 0),
+            (first_scales, 0),
             (quantize_h, 1),
             (quantize_wa, 0),
             (first_product, 0),

@@ -312,13 +312,7 @@ def tile_moe_elr_s_gelu_kernel(
                     copy(out=y_f32[span][:, 2 * half : 2 * half + 2, cols], in_=y_cols[e][half][:])
             if e == last - 1:
                 rows = out_0.rearrange("(p t) j -> p t j", t=PACK)[:, :, first * C : last * C]
-                if first == 0:
-                    for t in range(PACK):
-                        for half in range(2):
-                            part = slice(half * 4 * C, (half + 1) * 4 * C)
-                            nc.sync.dma_start(out=rows[:, t, part], in_=y_f32[span][:, t, part])
-                else:
-                    nc.sync.dma_start(out=rows, in_=y_f32[span][:])
+                nc.sync.dma_start(out=rows, in_=y_f32[span][:])
 
         def cast_y(e):
             span, cols = store_cols(e)
@@ -374,21 +368,21 @@ def tile_moe_elr_s_gelu_kernel(
         for stage, lag in (
             (cast_wa, 0),
             (quantize_h, 1),
+            (quantize_wb, 1),
+            (second_product, 1),
             (quantize_wa, 0),
             (first_product, 0),
             (cast_wb, 0),
+            (deal, 1),
             (gelu, 0),
-            (quantize_wb, 1),
-            (second_product, 1),
             (quantize_wb, 0),
             (quantize_h, 0),
             (second_product, 0),
-            (deal, 1),
             (empty, 1),
             (cast_y, 2),
             (quantize_y, 2),
-            (empty, 0),
             (cast_y, 1),
+            (empty, 0),
             (cast_y, 0),
             (quantize_y, 1),
             (quantize_y, 0),

from contextlib import ExitStack

import concourse.mybir as mybir
from concourse.masks import make_identity

K, T, E, C, H, N = 512, 768, 12, 128, 512, 512
FLOPS = 2 * E * C * (K * H + K * N + H * N)

F32 = mybir.dt.float32
BF16 = mybir.dt.bfloat16
I32 = mybir.dt.int32
U32 = mybir.dt.uint32
U16 = mybir.dt.uint16
U8 = mybir.dt.uint8
FP8X4 = mybir.dt.float8_e4m3fn_x4
FP4X4 = mybir.dt.float4_e2m1fn_x4
GELU = mybir.ActivationFunctionType.Gelu_apprx_tanh

P = 128
PACK = 4
QUADS = 4
QUAD = 32
LIST_COLS = C // 16
LAST = E - 1
WA_SLOTS, WB_SLOTS = 10, 8
FIRST_REUSED = 2
SLOT_BYTES = PACK * H * 4
AT_H_CODES, AT_WB_SCALES, AT_Y_BF, AT_WORDS, AT_SCALES = 0, 512, 1024, 2048, 4096
AT_FIRST_SCALES = 4608
AT_H_BF, AT_Y_DEALT = 0, 1024
GATHER = 4
VECTOR_COLS = 128
W_LOADS = ((0, 4), (4, 8), (8, 12))
STORES = ((0, 8), (8, 10), (10, 12))
PLANE_EXPERTS = 3


def span_of(spans, e):
    return [s for s in spans if s[0] <= e < s[1]][0]


def tile_moe_elr_s_gelu_kernel(
    tc, x_words, x_scales, w_words, w_scales, wa, wb, offs, out_0, out_1, out_2
):
    nc = tc.nc
    with ExitStack() as ctx:
        keep = ctx.enter_context(tc.tile_pool(name="keep", bufs=1))
        wa_ring = ctx.enter_context(tc.tile_pool(name="wa_ring", bufs=1))
        wb_ring = ctx.enter_context(tc.tile_pool(name="wb_ring", bufs=1))
        work = ctx.enter_context(tc.tile_pool(name="work", bufs=2))
        psum = ctx.enter_context(tc.psum_pool(name="psum", bufs=2))
        last_psum = ctx.enter_context(tc.psum_pool(name="last_psum", bufs=1))

        offsets = keep.tile([P, E * LIST_COLS], U16, name="offsets")
        tok_words = keep.tile([P, T], U32, name="tok_words", align_bytes=256)
        tok_scales = keep.tile([P, T], U8, name="tok_scales", align_bytes=256)
        w_planes = keep.tile([P, E, N], U8, name="w_planes", align_bytes=256)
        ident = keep.tile([P, P], F32, name="ident")
        y_planes = keep.tile([P, PLANE_EXPERTS * C], U8, name="y_planes", align_bytes=256)

        nc.gpsimd.memset(tok_scales[:].bitcast(I32), 0)
        nc.vector.memset(w_planes[:].bitcast(I32), 0)

        wa_raw, wb_raw, w_codes = {}, {}, {}

        def in_slot(ring, e, shape, dtype, name, at):
            if ring is wa_ring:
                slot = e if e < WA_SLOTS else e - WA_SLOTS + FIRST_REUSED
            else:
                slot = e % WB_SLOTS
            return ring.tile(
                shape, dtype, name="%s_%d" % (name, slot), align_bytes=256, offset=slot * SLOT_BYTES + at
            )

        def load_w(span):
            first, last = span
            w_codes[span] = keep.tile([P, last - first, 2 * N], U8, name="w_codes_%d" % first, align_bytes=256)
            nc.sync.dma_start(
                out=w_codes[span][:].bitcast(I32),
                in_=w_words[first:last, 0].rearrange("e p b -> p e b").bitcast(I32),
            )

        def load_wa(e):
            wa_raw[e] = in_slot(wa_ring, e, [P, PACK, H], F32, "wa_raw", 0)
            nc.sync.dma_start(out=wa_raw[e][:], in_=wa[e].rearrange("(p j) i -> p j i", j=PACK))

        def load_expert(e):
            if e > 0:
                load_wa(e)
            rows = wb[e].rearrange("(p j) n -> p j n", j=PACK)
            if e < LAST:
                wb_raw[e] = in_slot(wb_ring, e, [P, PACK, N], F32, "wb_raw", 0)
                nc.sync.dma_start(out=wb_raw[e][:], in_=rows)
            else:
                wb_raw[e] = []
                for half in range(2):
                    part = in_slot(
                        wb_ring, e, [P, PACK, N // 2], F32, "wb_half_%d" % half, half * SLOT_BYTES // 2
                    )
                    nc.sync.dma_start(out=part[:], in_=rows[:, :, half * N // 2 : (half + 1) * N // 2])
                    wb_raw[e].append(part)
            for span in W_LOADS:
                if e == max(span[0] - 1, 0):
                    load_w(span)

        nc.sync.dma_start(offsets[:], offs)
        nc.sync.dma_start(
            out=tok_words[:].bitcast(I32), in_=x_words[0].rearrange("p t d -> p (t d)").bitcast(I32)
        )
        load_wa(0)
        for r in range(4):
            nc.sync.dma_start(
                out=tok_scales[r:P:QUAD, :].bitcast(I32),
                in_=x_scales[0].rearrange("(q r) t -> r q t", r=4)[r].bitcast(I32),
            )
        load_expert(0)
        for r in range(4):
            nc.gpsimd.dma_start(
                out=w_planes[r:P:QUAD].bitcast(I32),
                in_=w_scales[:, 0].rearrange("e (q r) n -> r q e n", r=4)[r].bitcast(I32),
            )
        make_identity(nc, ident[:])
        for e in range(1, WB_SLOTS):
            load_expert(e)

        slot_words, slot_scales = {}, {}

        def gather_words(first, words):
            picks = offsets[:, first * LIST_COLS : (first + GATHER) * LIST_COLS]
            nc.vector.tensor_copy(words[:], tok_words[:].indirect(picks))
            for e in range(GATHER):
                slot_words[first + e] = words[:, e * C : (e + 1) * C].bitcast(FP8X4)

        def gather_scales(first, scales):
            picks = offsets[:, first * LIST_COLS : (first + GATHER) * LIST_COLS]
            nc.vector.tensor_copy(scales[:], tok_scales[:].indirect(picks))
            for e in range(GATHER):
                slot_scales[first + e] = scales[:, e * C : (e + 1) * C]

        def first_scales(e):
            if e == 0:
                gather_scales(0, in_slot(wa_ring, 0, [P, GATHER * C], U8, "first_scales", AT_FIRST_SCALES))

        def late_gather(e):
            first = (e + 1) * GATHER
            if first < E:
                gather_words(first, in_slot(wa_ring, e, [P, GATHER * C], U32, "slot_words", AT_WORDS))
                gather_scales(first, in_slot(wa_ring, e, [P, GATHER * C], U8, "slot_scales", AT_SCALES))

        wa_bf, wb_bf, h_bf, y_bf = {}, {}, {}, {}
        wa_q, wb_q, h_q = {}, {}, {}
        pre, y_rows, y_cols = {}, {}, {}
        y_f32, y_codes = {}, {}
        w_dealt = {}

        def quantize(values, codes, scales):
            nc.vector.quantize_mx(out=codes[:].bitcast(FP8X4), scales=scales[:], in_=values[:])
            return codes, scales

        def dealt(values):
            return values[:].rearrange("p (t m j) -> p m j t", t=PACK, j=PACK)

        def cast_wa(e):
            wa_bf[e] = work.tile([P, PACK * H], BF16, name="wa_bf", align_bytes=64)
            nc.vector.tensor_copy(
                out=dealt(wa_bf[e]), in_=wa_raw[e][:].rearrange("p j (m t) -> p m j t", t=PACK)
            )

        def cast_wb(e):
            wb_bf[e] = work.tile([P, PACK * N], BF16, name="wb_bf", align_bytes=64)
            if e < LAST:
                grouped = wb_bf[e][:].rearrange("p (c i j) -> p c j i", i=4, j=PACK)
                rows = wb_raw[e][:].rearrange("p j (c i) -> p c j i", i=4)
                cut = VECTOR_COLS // 4
                nc.vector.tensor_copy(out=grouped[:, :cut], in_=rows[:, :cut])
                nc.scalar.copy(out=grouped[:, cut:], in_=rows[:, cut:])
            else:
                for half, copy in enumerate((nc.scalar.copy, nc.vector.tensor_copy)):
                    copy(
                        out=dealt(wb_bf[e])[:, half * P // 2 : (half + 1) * P // 2],
                        in_=wb_raw[e][half][:].rearrange("p j (m t) -> p m j t", t=PACK),
                    )

        def deal_last_w():
            span = span_of(W_LOADS, LAST)
            words = keep.tile([P, 2 * N], U8, name="w_dealt_words", align_bytes=64)
            scales = keep.tile([P, N], U8, name="w_dealt_scales", align_bytes=64)
            nc.vector.tensor_copy(
                out=words[:].bitcast(U16).rearrange("p (t m) -> p t m", t=PACK),
                in_=w_codes[span][:, LAST - span[0], :].bitcast(U16).rearrange("p (m t) -> p t m", t=PACK),
            )
            nc.vector.tensor_copy(
                out=scales[:].rearrange("p (t m) -> p t m", t=PACK),
                in_=w_planes[:, LAST, :].rearrange("p (m t) -> p t m", t=PACK),
            )
            w_dealt[LAST] = words, scales

        def quantize_wa(e):
            codes = work.tile([P, H], U32, name="wa_codes", align_bytes=64)
            scales = work.tile([P, H], U8, name="wa_scales", align_bytes=64)
            wa_q[e] = quantize(wa_bf[e], codes, scales)

        def quantize_wb(e):
            codes = work.tile([P, N], U32, name="wb_codes", align_bytes=64)
            scales = in_slot(wa_ring, e + 1, [P, N], U8, "wb_scales", AT_WB_SCALES)
            wb_q[e] = quantize(wb_bf[e], codes, scales)

        def quantize_h(e):
            codes = in_slot(wa_ring, e + 1, [P, C], U32, "h_codes", AT_H_CODES)
            scales = work.tile([P, C], U8, name="h_scales", align_bytes=64)
            h_q[e] = quantize(h_bf[e], codes, scales)

        def first_product(e):
            codes, scales = wa_q[e]
            pre[e] = psum.tile([P, PACK, C], F32, name="pre")
            for t in range(PACK):
                cols = slice(t * P, (t + 1) * P)
                nc.tensor.matmul_mx(
                    out=pre[e][:, t, :],
                    lhsT=codes[:, cols].bitcast(FP8X4),
                    lhsT_scale=scales[:, cols],
                    rhs=slot_words[e],
                    rhs_scale=slot_scales[e],
                    start=True,
                    stop=True,
                )

        def gelu(e):
            h_bf[e] = in_slot(wb_ring, e, [P, C * PACK], BF16, "h_bf", AT_H_BF)
            nc.scalar.activation(
                out=h_bf[e][:].rearrange("p (u t) -> p u t", t=PACK),
                in_=pre[e][:].rearrange("p t u -> p u t"),
                func=GELU,
            )

        def second_product(e):
            if e == LAST:
                return last_product()
            w_span = span_of(W_LOADS, e)
            y_rows[e] = psum.tile([C, N], F32, name="y_rows")
            nc.tensor.matmul_mx(
                out=y_rows[e][:],
                lhsT=slot_words[e],
                lhsT_scale=slot_scales[e],
                rhs=w_codes[w_span][:, e - w_span[0], :].bitcast(FP4X4),
                rhs_scale=w_planes[:, e, :],
                start=True,
                stop=False,
            )
            nc.tensor.matmul_mx(
                out=y_rows[e][:],
                lhsT=h_q[e][0][:].bitcast(FP8X4),
                lhsT_scale=h_q[e][1][:],
                rhs=wb_q[e][0][:].bitcast(FP8X4),
                rhs_scale=wb_q[e][1][:],
                start=False,
                stop=True,
            )

        def last_product():
            words, scales = w_dealt[LAST]
            y_cols[LAST] = [last_psum.tile([P, 2, C], F32, name="y_last_%d" % half) for half in range(2)]
            for t in range(PACK):
                cols = slice(t * P, (t + 1) * P)
                nc.tensor.matmul_mx(
                    out=y_cols[LAST][t // 2][:, t % 2, :],
                    lhsT=words[:, 2 * t * P : 2 * (t + 1) * P].bitcast(FP4X4),
                    lhsT_scale=scales[:, cols],
                    rhs=slot_words[LAST],
                    rhs_scale=slot_scales[LAST],
                    start=t % 2 == 0,
                    stop=False,
                )
            for t in range(PACK):
                cols = slice(t * P, (t + 1) * P)
                nc.tensor.matmul_mx(
                    out=y_cols[LAST][t // 2][:, t % 2, :],
                    lhsT=wb_q[LAST][0][:, cols].bitcast(FP8X4),
                    lhsT_scale=wb_q[LAST][1][:, cols],
                    rhs=h_q[LAST][0][:].bitcast(FP8X4),
                    rhs_scale=h_q[LAST][1][:],
                    start=False,
                    stop=t % 2 == 1,
                )

        def deal(e):
            if e == LAST:
                return
            y_dealt = in_slot(wb_ring, e + 1, [C, PACK, P], F32, "y_dealt", AT_Y_DEALT)
            by_t = y_rows[e][:].rearrange("u (m t) -> u t m", t=PACK)
            for t in range(0, PACK, 2):
                nc.scalar.copy(out=y_dealt[:, t : t + 2, :], in_=by_t[:, t : t + 2, :])
            y_cols[e] = psum.tile([P, PACK, C], F32, name="y_cols")
            for t in range(PACK):
                nc.tensor.transpose(y_cols[e][:, t, :], y_dealt[:, t, :], ident[:])

        def store_cols(e):
            span = span_of(STORES, e)
            return span, slice((e - span[0]) * C, (e - span[0] + 1) * C)

        def empty(e):
            span, cols = store_cols(e)
            first, last = span
            if e == first:
                width = (last - first) * C
                y_f32[span] = keep.tile([P, PACK, width], F32, name="y_f32_%d" % first, align_bytes=256)
                y_codes[span] = keep.tile([P, width], U32, name="y_codes_%d" % first, align_bytes=256)
            if e < LAST:
                nc.scalar.copy(out=y_f32[span][:, :, cols], in_=y_cols[e][:])
            else:
                for half, copy in enumerate((nc.scalar.copy, nc.vector.tensor_copy)):
                    copy(out=y_f32[span][:, 2 * half : 2 * half + 2, cols], in_=y_cols[e][half][:])
            if e == last - 1:
                rows = out_0.rearrange("(p t) j -> p t j", t=PACK)[:, :, first * C : last * C]
                nc.sync.dma_start(out=rows, in_=y_f32[span][:])

        def cast_y(e):
            span, cols = store_cols(e)
            y_bf[e] = in_slot(wa_ring, e + 2, [P, C * PACK], BF16, "y_bf", AT_Y_BF)
            nc.vector.tensor_copy(
                out=y_bf[e][:].rearrange("p (c i t) -> p c t i", i=4, t=PACK),
                in_=y_f32[span][:, :, cols].rearrange("p t (c i) -> p c t i", i=4),
            )

        def quantize_y(e):
            span, cols = store_cols(e)
            first, last = span
            a, b = divmod(e, PLANE_EXPERTS)
            nc.vector.quantize_mx(
                out=y_codes[span][:, cols].bitcast(FP8X4),
                scales=y_planes[4 * a : P, b * C : (b + 1) * C],
                in_=y_bf[e][:],
            )
            if e == last - 1:
                nc.sync.dma_start(
                    out=out_1[0].rearrange("p j d -> p (j d)").bitcast(I32)[:, first * C : last * C],
                    in_=y_codes[span][:].bitcast(I32),
                )

        gather_words(0, keep.tile([P, GATHER * C], U32, name="first_words", align_bytes=64))

        stages = (
            (cast_wa, 0),
            (first_scales, 0),
            (quantize_h, 1),
            (quantize_wa, 0),
            (first_product, 0),
            (quantize_wb, 1),
            (second_product, 1),
            (cast_wb, 0),
            (cast_y, 2),
            (late_gather, 0),
            (quantize_y, 2),
            (deal, 1),
            (gelu, 0),
            (empty, 1),
        )
        for step in range(LAST):
            for stage, lag in stages:
                if 0 <= step - lag:
                    stage(step - lag)
            reload = step - 1 + WB_SLOTS
            if WB_SLOTS <= reload < E:
                load_expert(reload)
            if step == W_LOADS[-1][0]:
                deal_last_w()

        for stage, lag in (
            (cast_wa, 0),
            (quantize_h, 1),
            (quantize_wb, 1),
            (second_product, 1),
            (quantize_wa, 0),
            (first_product, 0),
            (cast_wb, 0),
            (deal, 1),
            (gelu, 0),
            (quantize_wb, 0),
            (quantize_h, 0),
            (second_product, 0),
            (empty, 1),
            (cast_y, 2),
            (quantize_y, 2),
            (cast_y, 1),
            (empty, 0),
            (cast_y, 0),
            (quantize_y, 1),
            (quantize_y, 0),
        ):
            stage(LAST - lag)

        for q in range(QUADS):
            nc.sync.dma_start(
                out=out_2[0, 4 * q : 4 * q + 4, :]
                .rearrange("r (a w) -> a r w", a=E // PLANE_EXPERTS)
                .bitcast(I32),
                in_=y_planes[QUAD * q : QUAD * q + 16, :].bitcast(I32),
            )
